import numpy as np, ml_dtypes
CORES = [1,17,65,89,97,113]
N = 6
import mx_ref
NC, G = 128, 2
C = np.float32(0.01674)
BF = ml_dtypes.bfloat16
def cut(t, i, w=512):
    return t[:, w * i:w * i + w]
def tile(rs):
    return np.stack(rs, axis=2).reshape(128, -1).astype(BF)
def layer(w, X):
    out = []
    for i in range(G):
        for t in range(len(X)):
            p = mx_ref.matmul(mx_ref.quantize(cut(w, len(X) * i + t)), X[t])
            z = p if t == 0 else z + p
        out.append(z)
    return out
def act(Z):
    return [np.maximum(s * z, 0) * C for z in Z for s in (1, -1)]
def setup_inputs(rng):
    def f(*shape):
        return mx_ref.flush((rng.standard_normal(shape, dtype=np.float32) * np.exp2(rng.integers(-2, 3, shape[:-1] + (1,)))).astype(BF))
    return {"x": f(N, 128, N * 4 * NC), "w1": f(N, 128, G * 512), "w2": f(N, 128, 2 * 512)}
def setup_inputs_blocks(rng):
    d = setup_inputs(rng)
    for k in ("x", "w1", "w2"): d[k] = mx_ref.spread(d[k], rng, 4)
    return d
def setup_inputs_wide(rng):
    d = setup_inputs(rng)
    for k in ("x", "w1", "w2"): d[k] = mx_ref.flush((d[k].astype(np.float32) * np.exp2(rng.integers(-6, 7, (N, 1, 1))).astype(np.float32)).astype(BF))
    return d
def reference(x, w1, w2, own=None):
    h = np.zeros((N, 128, 4 * NC), BF)
    for c in range(N):
        for j in range(N):
            P = layer(w1[j], [mx_ref.quantize(cut(x[j], c, 4 * NC))])
            Z = P if j == 0 else [z + p for z, p in zip(Z, P)]
        h[c] = tile(act(Z))
    use = h if own is None else own["h"]
    H = [mx_ref.quantize(use[j]) for j in range(N)]
    y = np.zeros((N, 128, NC), np.float32)
    for r in range(N):
        y[r] = mx_ref.matmul(mx_ref.quantize(cut(w2[r], 0)), H[r]) + mx_ref.matmul(mx_ref.quantize(cut(w2[r], 1)), H[(r + 1) % N])
    return {"h": h, "y": y}

@@ -1,0 +1,324 @@
+from concourse.mybir import dt, AluOpType, ActivationFunctionType
+
+NCORES = 128
+N = 6
+CACT = 0.01674
+W = 256
+
+SCRATCH = {
+    "xb": ("sbuf", [128, N * 512], "bfloat16"),
+    "w1b": ("sbuf", [128, 1024], "bfloat16"),
+    "w2b": ("sbuf", [128, 1024], "bfloat16"),
+    "xq": ("sbuf", [128, N * 128], "float8_e4m3fn_x4"),
+    "xs": ("sbuf", [128, N * 128], "uint8"),
+    "w1q": ("sbuf", [128, 256], "float8_e4m3fn_x4"),
+    "w1s": ("sbuf", [128, 256], "uint8"),
+    "w2q": ("sbuf", [128, 256], "float8_e4m3fn_x4"),
+    "w2s": ("sbuf", [128, 256], "uint8"),
+    "sb": ("sbuf", [128, N * W], "float32"),
+    "land": ("sbuf", [128, N * W], "float32"),
+    "zin": ("sbuf", [128, W], "float32"),
+    "acc": ("sbuf", [128, W], "float32"),
+    "ht": ("sbuf", [128, 512], "bfloat16"),
+    "hq": ("sbuf", [128, 128], "float8_e4m3fn_x4"),
+    "hs": ("sbuf", [128, 128], "uint8"),
+    "nq": ("sbuf", [128, 128], "float8_e4m3fn_x4"),
+    "ns": ("sbuf", [128, 128], "uint8"),
+    "yb": ("sbuf", [128, 128], "float32"),
+    "ps": ("psum", [128, 512 * 8], "float32"),
+}
+SEMAPHORES = (["ld_w1", "ld_w2", "qw1", "qw2", "zarr", "add", "z0", "z1", "a0", "a1", "a2", "a3", "qh", "nb",
+               "ymm", "ycp", "st_h", "st_y", "sentA", "sentB", "sentC"]
+              + ["ldx%d" % r for r in range(5)] + ["qx%d" % r for r in range(5)]
+              + ["mm%d_%d" % (r, i) for r in range(5) for i in range(2)]
+              + ["cpa%d" % c for c in range(N)] + ["cpb%d" % c for c in range(N)]
+              + ["arr%d" % c for c in range(N)])
+
+
+def _count(mask):
+    return bin(mask).count("1")
+
+
+def _plan(cores, topo):
+    n = len(cores)
+    q = [r for r in range(n) if not any(topo.may_write(cores[r], cores[j]) for j in range(n) if j != r)][0]
+    p = (q + 1) % n
+    rest = [j for j in range(n) if j != q]
+    free = [c for c in range(NCORES) if c not in cores]
+    qc = cores[q]
+    K = [c for c in free if topo.mates(topo.chip(c), topo.chip(qc)) and topo.may_write(c, qc)
+         and topo.die(c) == topo.die(cores[rest[0]]) and all(topo.may_write(cores[j], c) for j in rest)][0]
+    L = [c for c in free if topo.chip(c) == topo.chip(cores[p]) and topo.may_write(c, qc)
+         and topo.die(c) == topo.die(cores[p])][0]
+    own = [c for c in free if topo.chip(c) == topo.chip(qc) and topo.may_write(c, K)
+           and all(topo.may_write(c, cores[j]) for j in rest)]
+    near = [c for c in own if topo.die(c) == topo.die(qc)]
+    far = [c for c in own if topo.die(c) != topo.die(qc)]
+    relays = []
+    for a, b in zip(near, far):
+        relays += [a, b]
+    place = {c: cores[c] for c in range(n)}
+    place[q], place[p] = K, L
+    order = {}
+    for j in range(n):
+        o = [(j + s) % n for s in range(1, n)]
+        if j == q:
+            o = [q] + o
+        else:
+            if o[-1] in (q, p):
+                o.insert(0, o.pop())
+            if o[-1] in (q, p):
+                o[-2], o[-1] = o[-1], o[-2]
+            if j == p:
+                o.insert(1, p)
+        order[j] = o
+    relay_of = {c: relays[k % len(relays)] for k, c in enumerate(order[q])}
+    arrive = {}
+    for c in range(n):
+        ev = sorted((order[j].index(c) + (0.5 if j == p else 0.0), j) for j in rest if j != c)
+        ev = [j for _, j in ev]
+        if c in (q, p) or order[q].index(c) < 4:
+            ev.insert(len(ev) - 1, q)
+        else:
+            ev.append(q)
+        if c == p:
+            ev.insert(1, p)
+        arrive[c] = ev
+    return q, p, K, L, relays, place, order, relay_of, arrive
+
+
+def _runs(tiles):
+    groups = [tiles[0:1], tiles[1:3], tiles[3:]]
+    out = []
+    for gr in groups:
+        s = sorted(gr)
+        rs, cur = [], []
+        for t in s:
+            if cur and t != cur[-1] + 1:
+                rs.append(cur)
+                cur = []
+            cur.append(t)
+        if cur:
+            rs.append(cur)
+        rs.sort(key=lambda r: min(gr.index(t) for t in r))
+        out += [(r, [t for t in gr if t in r]) for r in rs]
+    return out
+
+
+def rank_program(g, core, T, topo):
+    cores = list(T.cores)
+    q, p, K, L, relays, place, order, relay_of, arrive = _plan(cores, topo)
+    rank = T.rank_of(core)
+    if rank is None and core not in (K, L) and core not in relays:
+        return
+    V, S, TE, SY = g.vector, g.scalar, g.tensor, g.sync
+    sem = T.sem
+    sent = {"sentA": 0, "sentB": 0, "sentC": 0}
+
+    def write(dst, out, in_, rsem, lsem, mask=None):
+        rid, pid, _ = topo.addr(dst)
+        m = topo.mask(core, dst) if mask is None else mask
+        g.remote_dma(out_ap=out, in_ap=in_, remote_sem=rsem, local_sem=sem[lsem], pid=pid, routing_id=rid,
+                     dma_engine_mask=m)
+        sent[lsem] += _count(m)
+
+    def slot(buf, c):
+        return buf[:, W * c:W * c + W]
+
+    def in_count(src, dst, mask=None):
+        return _count(topo.mask(src, dst) if mask is None else mask)
+
+    def finish_g():
+        for k in ("sentA", "sentB", "sentC"):
+            if sent[k]:
+                g.wait_ge(sem[k], sent[k])
+
+    off_mask = topo.mask(cores[p], K)
+    chip_only = topo.mask(cores[p], L) & ~off_mask
+
+    def arrival_count(c, j):
+        if j == q:
+            return in_count(relay_of[c], place[c])
+        if j == p and c == p:
+            return _count(chip_only)
+        return in_count(cores[j], place[c])
+
+    def make_tile(z, w0, w1):
+        for s_, v_ in w0:
+            S.wait_ge(s_, v_)
+        S.activation(T.ht[:, 0:512:4], z[:, 0:128], ActivationFunctionType.Relu, scale=CACT).then_inc(sem.a0, 1)
+        S.activation(T.ht[:, 1:512:4], z[:, 0:128], ActivationFunctionType.Relu, scale=-CACT).then_inc(sem.a1, 1)
+        for s_, v_ in w1:
+            S.wait_ge(s_, v_)
+            V.wait_ge(s_, v_)
+        V.tensor_scalar(T.ht[:, 2:512:4], z[:, 128:256], 0.0, CACT, AluOpType.max, AluOpType.mult).then_inc(sem.a2, 1)
+        S.activation(T.ht[:, 3:512:4], z[:, 128:256], ActivationFunctionType.Relu, scale=-CACT).then_inc(sem.a3, 1)
+        for a in (sem.a0, sem.a1, sem.a2, sem.a3):
+            V.wait_ge(a, 1)
+        V.quantize_mx(T.hq[:, 0:128], T.hs[:, 0:128], T.ht[:, 0:512]).then_inc(sem.qh, 1)
+
+    def sum_tile(c, last_psum=None, hook=None):
+        src = arrive[c]
+        n_land = len(src) if last_psum else len(src) - 1
+        done = 0
+        for k in range(1, n_land):
+            if hook and k == n_land - 1:
+                hook()
+            if k == 1:
+                V.wait_ge(sem["arr%d" % src[0]], arrival_count(c, src[0]))
+            V.wait_ge(sem["arr%d" % src[k]], arrival_count(c, src[k]))
+            if done:
+                V.wait_ge(sem.add, done)
+            a = slot(T.land, src[0]) if k == 1 else T.acc[:, 0:W]
+            V.tensor_tensor(T.acc[:, 0:W], a, slot(T.land, src[k]), AluOpType.add).then_inc(sem.add, 1)
+            done += 1
+        V.wait_ge(sem.add, done)
+        if last_psum:
+            halves, waits = last_psum
+        else:
+            j = src[-1]
+            halves = (T.land[:, W * j:W * j + 128], T.land[:, W * j + 128:W * j + W])
+            waits = ((sem["arr%d" % j], arrival_count(c, j)),) * 2
+        for i, zs in enumerate((sem.z0, sem.z1)):
+            V.wait_ge(waits[i][0], waits[i][1])
+            V.tensor_tensor(T.acc[:, 128 * i:128 * i + 128], T.acc[:, 128 * i:128 * i + 128], halves[i],
+                            AluOpType.add).then_inc(zs, 1)
+        make_tile(T.acc, [(sem.z0, 1)], [(sem.z1, 1)])
+
+    def send_codes(dst, lsem):
+        g.wait_ge(sem.qh, 1)
+        write(dst, T.nq[:, 0:128].bitcast(dt.uint8), T.hq[:, 0:128].bitcast(dt.uint8), sem.nb, lsem)
+        write(dst, T.ns[:, 0:128], T.hs[:, 0:128], sem.nb, lsem)
+
+    if core in relays:
+        for c in order[q]:
+            if relay_of[c] == core:
+                g.wait_ge(sem["arr%d" % c], in_count(cores[q], core))
+                write(place[c], slot(T.land, q), slot(T.land, c), sem["arr%d" % q], "sentB")
+        finish_g()
+        return
+
+    if core in (K, L):
+        c = q if core == K else p
+        sum_tile(c)
+        g.wait_ge(sem.z0, 1)
+        g.wait_ge(sem.z1, 1)
+        write(cores[c], T.zin[:, 0:W], T.acc[:, 0:W], sem.zarr, "sentB", off_mask)
+        send_codes(cores[(c - 1) % N], "sentB")
+        finish_g()
+        return
+
+    summed_here = place[rank] == core
+    tiles = order[rank]
+    runs = _runs(tiles)
+    if summed_here:
+        runs = runs + [([rank], [])]
+    n_first = len(runs) - (1 if summed_here else 0)
+
+    def load_x(queue, r):
+        a, b = runs[r][0][0], runs[r][0][-1] + 1
+        queue.dma_start(T.xb[:, 512 * a:512 * b], T.x[:, 512 * a:512 * b]).then_inc(sem["ldx%d" % r], 16)
+
+    SY.dma_start(T.w1b[:, 0:1024], T.w1[:, 0:1024]).then_inc(sem.ld_w1, 16)
+    for r in range(n_first):
+        load_x(S if r % 2 == 0 else SY, r)
+
+    readers = {}
+    bank = {}
+
+    def quant_run(r):
+        a, b = runs[r][0][0], runs[r][0][-1] + 1
+        V.wait_ge(sem["ldx%d" % r], 16)
+        V.quantize_mx(T.xq[:, 128 * a:128 * b], T.xs[:, 128 * a:128 * b], T.xb[:, 512 * a:512 * b]).then_inc(sem["qx%d" % r], 1)
+
+    def mult_run(r):
+        a, b = runs[r][0][0], runs[r][0][-1] + 1
+        TE.wait_ge(sem["qx%d" % r], 1)
+        for i in range(2):
+            bk = (2 * r + i) % 8
+            for s_ in readers.get(bk, []):
+                TE.wait_ge(s_, 1)
+            readers[bk] = []
+            bank[(r, i)] = bk
+            TE.matmul_mx(T.ps[:, 512 * bk:512 * bk + 128 * (b - a)], T.w1q[:, 128 * i:128 * i + 128],
+                         T.w1s[:, 128 * i:128 * i + 128], T.xq[:, 128 * a:128 * b], T.xs[:, 128 * a:128 * b],
+                         True, True).then_inc(sem["mm%d_%d" % (r, i)], 1)
+
+    V.wait_ge(sem.ld_w1, 16)
+    V.quantize_mx(T.w1q[:, 0:256], T.w1s[:, 0:256], T.w1b[:, 0:1024]).then_inc(sem.qw1, 1)
+    TE.wait_ge(sem.qw1, 1)
+    for r in range(n_first):
+        quant_run(r)
+        mult_run(r)
+        V.wait_ge(sem["mm%d_0" % r], 1)
+        S.wait_ge(sem["mm%d_1" % r], 1)
+        for c in runs[r][1]:
+            o = 128 * (c - runs[r][0][0])
+            b0, b1 = bank[(r, 0)], bank[(r, 1)]
+            V.tensor_copy(T.sb[:, W * c:W * c + 128], T.ps[:, 512 * b0 + o:512 * b0 + o + 128]).then_inc(sem["cpa%d" % c], 1)
+            S.activation(T.sb[:, W * c + 128:W * c + W], T.ps[:, 512 * b1 + o:512 * b1 + o + 128],
+                         ActivationFunctionType.Copy).then_inc(sem["cpb%d" % c], 1)
+            readers[b0].append(sem["cpa%d" % c])
+            readers[b1].append(sem["cpb%d" % c])
+
+    for k, c in enumerate(tiles):
+        g.wait_ge(sem["cpa%d" % c], 1)
+        g.wait_ge(sem["cpb%d" % c], 1)
+        ls = "sentA" if k < len(tiles) - 2 else "sentB"
+        if rank == q:
+            write(relay_of[c], slot(T.land, c), slot(T.sb, c), sem["arr%d" % c], ls)
+        elif c == rank:
+            write(place[c], slot(T.land, rank), slot(T.sb, c), sem["arr%d" % rank], ls, chip_only)
+        else:
+            write(place[c], slot(T.land, rank), slot(T.sb, c), sem["arr%d" % rank], ls)
+
+    SY.wait_ge(sem.sentA, sent["sentA"])
+    if summed_here:
+        load_x(SY, n_first)
+    SY.dma_start(T.w2b[:, 0:1024], T.w2[:, 0:1024]).then_inc(sem.ld_w2, 16)
+
+    def quant_w2():
+        V.wait_ge(sem.ld_w2, 16)
+        V.quantize_mx(T.w2q[:, 0:256], T.w2s[:, 0:256], T.w2b[:, 0:1024]).then_inc(sem.qw2, 1)
+
+    if summed_here:
+        r = n_first
+        mult_run(r)
+        b0, b1 = bank[(r, 0)], bank[(r, 1)]
+        sum_tile(rank,
+                 last_psum=((T.ps[:, 512 * b0:512 * b0 + 128], T.ps[:, 512 * b1:512 * b1 + 128]),
+                            ((sem["mm%d_0" % r], 1), (sem["mm%d_1" % r], 1))),
+                 hook=lambda: quant_run(r))
+        quant_w2()
+        send_codes(cores[(rank - 1) % N], "sentC")
+    else:
+        quant_w2()
+        n_z = _count(off_mask)
+        make_tile(T.zin, [(sem.zarr, n_z)], [(sem.zarr, n_z)])
+
+    for a in (sem.a0, sem.a1, sem.a2, sem.a3):
+        SY.wait_ge(a, 1)
+    if sent["sentC"]:
+        SY.wait_ge(sem.sentC, sent["sentC"])
+    SY.dma_start(T.h[:, 0:512], T.ht[:, 0:512]).then_inc(sem.st_h, 16)
+
+    yb = (2 * len(runs)) % 8
+    for s_ in readers.get(yb, []):
+        TE.wait_ge(s_, 1)
+    nxt = (rank + 1) % N
+    src = K if nxt == q else (L if nxt == p else cores[nxt])
+    TE.wait_ge(sem.qw2, 1)
+    TE.wait_ge(sem.qh, 1)
+    TE.matmul_mx(T.ps[:, 512 * yb:512 * yb + 128], T.w2q[:, 0:128], T.w2s[:, 0:128], T.hq[:, 0:128], T.hs[:, 0:128],
+                 True, False)
+    TE.wait_ge(sem.nb, 2 * in_count(src, core))
+    TE.matmul_mx(T.ps[:, 512 * yb:512 * yb + 128], T.w2q[:, 128:256], T.w2s[:, 128:256], T.nq[:, 0:128], T.ns[:, 0:128],
+                 False, True).then_inc(sem.ymm, 1)
+    S.wait_ge(sem.ymm, 1)
+    S.activation(T.yb[:, 0:128], T.ps[:, 512 * yb:512 * yb + 128], ActivationFunctionType.Copy).then_inc(sem.ycp, 1)
+    S.wait_ge(sem.ycp, 1)
+    S.dma_start(T.y[:, 0:128], T.yb[:, 0:128]).then_inc(sem.st_y, 16)
+
+    finish_g()
+    g.wait_ge(sem.st_h, 16)
+    g.wait_ge(sem.st_y, 16)

@@ -19,16 +19,22 @@ SCRATCH = {
     "land": ("sbuf", [128, N * W], "float32"),
     "zin": ("sbuf", [128, W], "float32"),
     "acc": ("sbuf", [128, W], "float32"),
+    "acc2": ("sbuf", [128, W], "float32"),
     "ht": ("sbuf", [128, 512], "bfloat16"),
     "hq": ("sbuf", [128, 128], "float8_e4m3fn_x4"),
     "hs": ("sbuf", [128, 128], "uint8"),
     "nq": ("sbuf", [128, 128], "float8_e4m3fn_x4"),
     "ns": ("sbuf", [128, 128], "uint8"),
     "yb": ("sbuf", [128, 128], "float32"),
+    "gw1q": ("sbuf", [128, 256], "float8_e4m3fn_x4"),
+    "gw1s": ("sbuf", [128, 256], "uint8"),
+    "gxq": ("sbuf", [128, 128], "float8_e4m3fn_x4"),
+    "gxs": ("sbuf", [128, 128], "uint8"),
     "ps": ("psum", [128, 512 * 8], "float32"),
 }
 SEMAPHORES = (["ld_w1", "ld_w2", "qw1", "qw2", "zarr", "add", "z0", "z1", "a0", "a1", "a2", "a3", "qh", "nb",
-               "ymm", "ycp", "st_h", "st_y", "sentA", "sentB", "sentC"]
+               "ymm", "ycp", "st_h", "st_y", "sentA", "sentB", "sentC", "sentD", "ldxt", "qxt", "hpiece", "gift", "rsum",
+               "ld_w1b", "qw1b", "arh"]
               + ["ldx%d" % r for r in range(5)] + ["qx%d" % r for r in range(5)]
               + ["mm%d_%d" % (r, i) for r in range(5) for i in range(2)]
               + ["cpa%d" % c for c in range(N)] + ["cpb%d" % c for c in range(N)]
@@ -59,32 +65,25 @@ def _plan(cores, topo):
         relays += [a, b]
     place = {c: cores[c] for c in range(n)}
     place[q], place[p] = K, L
-    order = {}
-    for j in range(n):
-        o = [(j + s) % n for s in range(1, n)]
-        if j == q:
-            o = [q] + o
-        else:
-            if o[-1] in (q, p):
-                o.insert(0, o.pop())
-            if o[-1] in (q, p):
-                o[-2], o[-1] = o[-1], o[-2]
-            if j == p:
-                o.insert(1, p)
-        order[j] = o
+    ring = [j for j in rest if j != p]
+    taker = {ring[k]: ring[(k + 1) % len(ring)] for k in range(len(ring))}
+    giver = {t: a for a, t in taker.items()}
+    helpers = {a: [c for c in free if c not in (K, L) and c not in relays and topo.chip(c) == topo.chip(cores[a])
+                   and topo.die(c) != topo.die(cores[a]) and topo.may_write(c, cores[taker[a]])][:4] for a in ring}
+    r0, r1, r2, r3 = ring
+    order = {r0: [q, p, r3, r2], r1: [p, q, r0, r3], r2: [r1, q, p, r0], r3: [r2, p, q, r1],
+             p: [q, r0, p, r3, r1, r2], q: [q] + [(q + s) % n for s in range(1, n)]}
     relay_of = {c: relays[k % len(relays)] for k, c in enumerate(order[q])}
     arrive = {}
     for c in range(n):
-        ev = sorted((order[j].index(c) + (0.5 if j == p else 0.0), j) for j in rest if j != c)
-        ev = [j for _, j in ev]
-        if c in (q, p) or order[q].index(c) < 4:
-            ev.insert(len(ev) - 1, q)
-        else:
-            ev.append(q)
-        if c == p:
-            ev.insert(1, p)
-        arrive[c] = ev
-    return q, p, K, L, relays, place, order, relay_of, arrive
+        ev = []
+        for j in range(n):
+            if c in order[j]:
+                k = order[j].index(c)
+                ev.append((0.5 * k + 2.5 if j == q else (2.5 if (j == p and c == q) else float(k)), j))
+        arrive[c] = [j for _, j in sorted(ev)]
+    arrive[q] = [j for j in arrive[q] if j not in (p, q)] + [p, q]
+    return q, p, K, L, relays, place, order, relay_of, arrive, taker, giver, helpers
 
 
 def _runs(tiles):
@@ -107,13 +106,14 @@ def _runs(tiles):
 
 def rank_program(g, core, T, topo):
     cores = list(T.cores)
-    q, p, K, L, relays, place, order, relay_of, arrive = _plan(cores, topo)
+    q, p, K, L, relays, place, order, relay_of, arrive, taker, giver, helpers = _plan(cores, topo)
     rank = T.rank_of(core)
-    if rank is None and core not in (K, L) and core not in relays:
+    piece_of = {h: (a, k) for a in helpers for k, h in enumerate(helpers[a])}
+    if rank is None and core not in (K, L) and core not in relays and core not in piece_of:
         return
     V, S, TE, SY = g.vector, g.scalar, g.tensor, g.sync
     sem = T.sem
-    sent = {"sentA": 0, "sentB": 0, "sentC": 0}
+    sent = {"sentA": 0, "sentB": 0, "sentC": 0, "sentD": 0}
 
     def write(dst, out, in_, rsem, lsem, mask=None):
         rid, pid, _ = topo.addr(dst)
@@ -125,22 +125,31 @@ def rank_program(g, core, T, topo):
     def slot(buf, c):
         return buf[:, W * c:W * c + W]
 
+    def half(buf, c, i):
+        return buf[:, W * c + 128 * i:W * c + 128 * i + 128]
+
     def in_count(src, dst, mask=None):
         return _count(topo.mask(src, dst) if mask is None else mask)
 
     def finish_g():
-        for k in ("sentA", "sentB", "sentC"):
+        for k in ("sentA", "sentB", "sentC", "sentD"):
             if sent[k]:
                 g.wait_ge(sem[k], sent[k])
 
     off_mask = topo.mask(cores[p], K)
     chip_only = topo.mask(cores[p], L) & ~off_mask
+    lanes = [chip_only, off_mask]
+
+    def lane_of(k, i=0):
+        return lanes[i] if k == 0 else lanes[(k + 1) % 2]
 
     def arrival_count(c, j):
         if j == q:
-            return in_count(relay_of[c], place[c])
+            return in_count(relay_of[c], place[c]) * (2 if c == order[q][0] else 1)
         if j == p and c == p:
             return _count(chip_only)
+        if j == p and c == q:
+            return in_count(L, K)
         return in_count(cores[j], place[c])
 
     def make_tile(z, w0, w1):
@@ -157,13 +166,11 @@ def rank_program(g, core, T, topo):
             V.wait_ge(a, 1)
         V.quantize_mx(T.hq[:, 0:128], T.hs[:, 0:128], T.ht[:, 0:512]).then_inc(sem.qh, 1)
 
-    def sum_tile(c, last_psum=None, hook=None):
+    def sum_tile(c, last_psum=None):
         src = arrive[c]
         n_land = len(src) if last_psum else len(src) - 1
         done = 0
         for k in range(1, n_land):
-            if hook and k == n_land - 1:
-                hook()
             if k == 1:
                 V.wait_ge(sem["arr%d" % src[0]], arrival_count(c, src[0]))
             V.wait_ge(sem["arr%d" % src[k]], arrival_count(c, src[k]))
@@ -185,21 +192,73 @@ def rank_program(g, core, T, topo):
                             AluOpType.add).then_inc(zs, 1)
         make_tile(T.acc, [(sem.z0, 1)], [(sem.z1, 1)])
 
+    def close_q(base, own):
+        V.tensor_tensor(T.acc2[:, 0:W], base, slot(T.land, p), AluOpType.add).then_inc(sem.rsum, 1)
+        V.wait_ge(sem.rsum, 1)
+        for s_, v_ in own[1]:
+            V.wait_ge(s_, v_)
+        for i, zs in enumerate((sem.z0, sem.z1)):
+            V.tensor_tensor(T.acc2[:, 128 * i:128 * i + 128], T.acc2[:, 128 * i:128 * i + 128],
+                            own[0][:, 128 * i:128 * i + 128], AluOpType.add).then_inc(zs, 1)
+        make_tile(T.acc2, [(sem.z0, 1)], [(sem.z1, 1)])
+
     def send_codes(dst, lsem):
         g.wait_ge(sem.qh, 1)
         write(dst, T.nq[:, 0:128].bitcast(dt.uint8), T.hq[:, 0:128].bitcast(dt.uint8), sem.nb, lsem)
         write(dst, T.ns[:, 0:128], T.hs[:, 0:128], sem.nb, lsem)
 
-    if core in relays:
-        for c in order[q]:
-            if relay_of[c] == core:
-                g.wait_ge(sem["arr%d" % c], in_count(cores[q], core))
-                write(place[c], slot(T.land, q), slot(T.land, c), sem["arr%d" % q], "sentB")
+    def pieces(xcol):
+        return [(T.gw1q[:, 0:256].bitcast(dt.uint8), T.w1q[:, 0:256].bitcast(dt.uint8)),
+                (T.gw1s[:, 0:256], T.w1s[:, 0:256]),
+                (T.gxq[:, 0:128].bitcast(dt.uint8), T.xq[:, xcol:xcol + 128].bitcast(dt.uint8)),
+                (T.gxs[:, 0:128], T.xs[:, xcol:xcol + 128])]
+
+    if core in piece_of:
+        a, k = piece_of[core]
+        buf = pieces(0)[k][0]
+        g.wait_ge(sem.hpiece, _count(chip_only))
+        write(cores[taker[a]], buf, buf, sem.gift, "sentB")
         finish_g()
         return
 
-    if core in (K, L):
-        c = q if core == K else p
+    if core in relays:
+        for k, c in enumerate(order[q]):
+            if relay_of[c] == core:
+                if k == 0:
+                    g.wait_ge(sem.arh, _count(lane_of(0, 0)))
+                    write(place[c], half(T.land, q, 0), half(T.land, c, 0), sem["arr%d" % q], "sentB")
+                    g.wait_ge(sem["arr%d" % c], _count(lane_of(0, 1)))
+                    write(place[c], half(T.land, q, 1), half(T.land, c, 1), sem["arr%d" % q], "sentB")
+                else:
+                    g.wait_ge(sem["arr%d" % c], _count(lane_of(k)))
+                    write(place[c], slot(T.land, q), slot(T.land, c), sem["arr%d" % q], "sentB")
+        finish_g()
+        return
+
+    if core == K:
+        src = arrive[q][:-2]
+        for k in range(1, len(src)):
+            if k == 1:
+                V.wait_ge(sem["arr%d" % src[0]], arrival_count(q, src[0]))
+            V.wait_ge(sem["arr%d" % src[k]], arrival_count(q, src[k]))
+            if k > 1:
+                V.wait_ge(sem.add, k - 1)
+            a = slot(T.land, src[0]) if k == 1 else T.acc[:, 0:W]
+            V.tensor_tensor(T.acc[:, 0:W], a, slot(T.land, src[k]), AluOpType.add).then_inc(sem.add, 1)
+        g.wait_ge(sem.add, len(src) - 1)
+        write(cores[q], T.zin[:, 0:W], T.acc[:, 0:W], sem.zarr, "sentB", off_mask)
+        V.wait_ge(sem.add, len(src) - 1)
+        V.wait_ge(sem["arr%d" % p], arrival_count(q, p))
+        close_q(T.acc[:, 0:W], (slot(T.land, q), [(sem["arr%d" % q], arrival_count(q, q))]))
+        send_codes(cores[(q - 1) % N], "sentB")
+        finish_g()
+        return
+
+    if core == L:
+        c = p
+        g.wait_ge(sem.zarr, _count(chip_only))
+        write(K, slot(T.land, p), T.zin[:, 0:W], sem["arr%d" % p], "sentB")
+        write(cores[q], slot(T.land, p), T.zin[:, 0:W], sem["arr%d" % p], "sentB")
         sum_tile(c)
         g.wait_ge(sem.z0, 1)
         g.wait_ge(sem.z1, 1)
@@ -219,9 +278,19 @@ def rank_program(g, core, T, topo):
         a, b = runs[r][0][0], runs[r][0][-1] + 1
         queue.dma_start(T.xb[:, 512 * a:512 * b], T.x[:, 512 * a:512 * b]).then_inc(sem["ldx%d" % r], 16)
 
-    SY.dma_start(T.w1b[:, 0:1024], T.w1[:, 0:1024]).then_inc(sem.ld_w1, 16)
-    for r in range(n_first):
-        load_x(S if r % 2 == 0 else SY, r)
+    if rank == q:
+        SY.dma_start(T.w1b[:, 0:512], T.w1[:, 0:512]).then_inc(sem.ld_w1, 16)
+        load_x(S, 0)
+        SY.dma_start(T.w1b[:, 512:1024], T.w1[:, 512:1024]).then_inc(sem.ld_w1b, 16)
+        for r in range(1, len(runs)):
+            load_x(S if r % 2 == 1 else SY, r)
+    else:
+        SY.dma_start(T.w1b[:, 0:1024], T.w1[:, 0:1024]).then_inc(sem.ld_w1, 16)
+        if summed_here:
+            t = taker[rank]
+            S.dma_start(T.xb[:, 512 * t:512 * t + 512], T.x[:, 512 * t:512 * t + 512]).then_inc(sem.ldxt, 16)
+        for r in range(len(runs)):
+            load_x((S if r % 2 == 0 else SY) if not summed_here else (SY if r % 2 == 0 else S), r)
 
     readers = {}
     bank = {}
@@ -240,41 +309,73 @@ def rank_program(g, core, T, topo):
                 TE.wait_ge(s_, 1)
             readers[bk] = []
             bank[(r, i)] = bk
+            if rank == q and i == 1:
+                TE.wait_ge(sem.qw1b, 1)
             TE.matmul_mx(T.ps[:, 512 * bk:512 * bk + 128 * (b - a)], T.w1q[:, 128 * i:128 * i + 128],
                          T.w1s[:, 128 * i:128 * i + 128], T.xq[:, 128 * a:128 * b], T.xs[:, 128 * a:128 * b],
                          True, True).then_inc(sem["mm%d_%d" % (r, i)], 1)
 
     V.wait_ge(sem.ld_w1, 16)
-    V.quantize_mx(T.w1q[:, 0:256], T.w1s[:, 0:256], T.w1b[:, 0:1024]).then_inc(sem.qw1, 1)
+    if rank == q:
+        V.quantize_mx(T.w1q[:, 0:128], T.w1s[:, 0:128], T.w1b[:, 0:512]).then_inc(sem.qw1, 1)
+        quant_run(0)
+        V.wait_ge(sem.ld_w1b, 16)
+        V.quantize_mx(T.w1q[:, 128:256], T.w1s[:, 128:256], T.w1b[:, 512:1024]).then_inc(sem.qw1b, 1)
+    else:
+        V.quantize_mx(T.w1q[:, 0:256], T.w1s[:, 0:256], T.w1b[:, 0:1024]).then_inc(sem.qw1, 1)
     TE.wait_ge(sem.qw1, 1)
+    if summed_here:
+        t = taker[rank]
+        V.wait_ge(sem.ldxt, 16)
+        V.quantize_mx(T.xq[:, 128 * t:128 * t + 128], T.xs[:, 128 * t:128 * t + 128],
+                      T.xb[:, 512 * t:512 * t + 512]).then_inc(sem.qxt, 1)
+        g.wait_ge(sem.qw1, 1)
+        gift = pieces(128 * t)
+        for k in (0, 2, 1, 3):
+            if k == 2:
+                g.wait_ge(sem.qxt, 1)
+            write(helpers[rank][k], gift[k][0], gift[k][1], sem.hpiece, "sentD", chip_only)
     for r in range(n_first):
-        quant_run(r)
+        early = rank == q and r == 0
+        if not early:
+            quant_run(r)
         mult_run(r)
-        V.wait_ge(sem["mm%d_0" % r], 1)
-        S.wait_ge(sem["mm%d_1" % r], 1)
+        (S if early else V).wait_ge(sem["mm%d_0" % r], 1)
+        if not early:
+            S.wait_ge(sem["mm%d_1" % r], 1)
         for c in runs[r][1]:
             o = 128 * (c - runs[r][0][0])
             b0, b1 = bank[(r, 0)], bank[(r, 1)]
-            V.tensor_copy(T.sb[:, W * c:W * c + 128], T.ps[:, 512 * b0 + o:512 * b0 + o + 128]).then_inc(sem["cpa%d" % c], 1)
+            if early:
+                S.activation(T.sb[:, W * c:W * c + 128], T.ps[:, 512 * b0 + o:512 * b0 + o + 128],
+                             ActivationFunctionType.Copy).then_inc(sem["cpa%d" % c], 1)
+                S.wait_ge(sem["mm%d_1" % r], 1)
+            else:
+                V.tensor_copy(T.sb[:, W * c:W * c + 128], T.ps[:, 512 * b0 + o:512 * b0 + o + 128]).then_inc(sem["cpa%d" % c], 1)
             S.activation(T.sb[:, W * c + 128:W * c + W], T.ps[:, 512 * b1 + o:512 * b1 + o + 128],
                          ActivationFunctionType.Copy).then_inc(sem["cpb%d" % c], 1)
             readers[b0].append(sem["cpa%d" % c])
             readers[b1].append(sem["cpb%d" % c])
 
     for k, c in enumerate(tiles):
-        g.wait_ge(sem["cpa%d" % c], 1)
-        g.wait_ge(sem["cpb%d" % c], 1)
         ls = "sentA" if k < len(tiles) - 2 else "sentB"
+        g.wait_ge(sem["cpa%d" % c], 1)
+        if rank == q and k == 0:
+            write(relay_of[c], half(T.land, c, 0), half(T.sb, c, 0), sem.arh, ls, lane_of(0, 0))
+            g.wait_ge(sem["cpb%d" % c], 1)
+            write(relay_of[c], half(T.land, c, 1), half(T.sb, c, 1), sem["arr%d" % c], ls, lane_of(0, 1))
+            continue
+        g.wait_ge(sem["cpb%d" % c], 1)
         if rank == q:
-            write(relay_of[c], slot(T.land, c), slot(T.sb, c), sem["arr%d" % c], ls)
+            write(relay_of[c], slot(T.land, c), slot(T.sb, c), sem["arr%d" % c], ls, lane_of(k))
+        elif rank == p and c == q:
+            write(L, T.zin[:, 0:W], slot(T.sb, c), sem.zarr, ls, chip_only)
         elif c == rank:
             write(place[c], slot(T.land, rank), slot(T.sb, c), sem["arr%d" % rank], ls, chip_only)
         else:
             write(place[c], slot(T.land, rank), slot(T.sb, c), sem["arr%d" % rank], ls)
 
     SY.wait_ge(sem.sentA, sent["sentA"])
-    if summed_here:
-        load_x(SY, n_first)
     SY.dma_start(T.w2b[:, 0:1024], T.w2[:, 0:1024]).then_inc(sem.ld_w2, 16)
 
     def quant_w2():
@@ -283,14 +384,32 @@ def rank_program(g, core, T, topo):
 
     if summed_here:
         r = n_first
-        mult_run(r)
+        quant_run(r)
+        TE.wait_ge(sem["qx%d" % r], 1)
+        for i in range(2):
+            bk = (2 * r + i) % 8
+            for s_ in readers.get(bk, []):
+                TE.wait_ge(s_, 1)
+            readers[bk] = []
+            bank[(r, i)] = bk
+            TE.matmul_mx(T.ps[:, 512 * bk:512 * bk + 128], T.w1q[:, 128 * i:128 * i + 128], T.w1s[:, 128 * i:128 * i + 128],
+                         T.xq[:, 128 * rank:128 * rank + 128], T.xs[:, 128 * rank:128 * rank + 128], True, False)
+        TE.wait_ge(sem.gift, sum(in_count(h_, core) for h_ in helpers[giver[rank]]))
+        for i in range(2):
+            bk = bank[(r, i)]
+            TE.matmul_mx(T.ps[:, 512 * bk:512 * bk + 128], T.gw1q[:, 128 * i:128 * i + 128], T.gw1s[:, 128 * i:128 * i + 128],
+                         T.gxq[:, 0:128], T.gxs[:, 0:128], False, True).then_inc(sem["mm%d_%d" % (r, i)], 1)
         b0, b1 = bank[(r, 0)], bank[(r, 1)]
         sum_tile(rank,
                  last_psum=((T.ps[:, 512 * b0:512 * b0 + 128], T.ps[:, 512 * b1:512 * b1 + 128]),
-                            ((sem["mm%d_0" % r], 1), (sem["mm%d_1" % r], 1))),
-                 hook=lambda: quant_run(r))
+                            ((sem["mm%d_0" % r], 1), (sem["mm%d_1" % r], 1))))
         quant_w2()
         send_codes(cores[(rank - 1) % N], "sentC")
+    elif rank == q:
+        quant_w2()
+        V.wait_ge(sem.zarr, _count(off_mask))
+        V.wait_ge(sem["arr%d" % p], in_count(L, core))
+        close_q(T.zin[:, 0:W], (slot(T.sb, q), [(sem["cpa%d" % q], 1), (sem["cpb%d" % q], 1)]))
     else:
         quant_w2()
         n_z = _count(off_mask)

from concourse.mybir import dt, AluOpType, ActivationFunctionType

NCORES = 128
N = 6
CACT = 0.01674
W = 256

SCRATCH = {
    "xb": ("sbuf", [128, N * 512], "bfloat16"),
    "w1b": ("sbuf", [128, 1024], "bfloat16"),
    "w2b": ("sbuf", [128, 1024], "bfloat16"),
    "xq": ("sbuf", [128, N * 128], "float8_e4m3fn_x4"),
    "xs": ("sbuf", [128, N * 128], "uint8"),
    "w1q": ("sbuf", [128, 256], "float8_e4m3fn_x4"),
    "w1s": ("sbuf", [128, 256], "uint8"),
    "w2q": ("sbuf", [128, 256], "float8_e4m3fn_x4"),
    "w2s": ("sbuf", [128, 256], "uint8"),
    "sb": ("sbuf", [128, N * W], "float32"),
    "land": ("sbuf", [128, N * W], "float32"),
    "zin": ("sbuf", [128, W], "float32"),
    "acc": ("sbuf", [128, W], "float32"),
    "acc2": ("sbuf", [128, W], "float32"),
    "ht": ("sbuf", [128, 512], "bfloat16"),
    "hq": ("sbuf", [128, 128], "float8_e4m3fn_x4"),
    "hs": ("sbuf", [128, 128], "uint8"),
    "nq": ("sbuf", [128, 128], "float8_e4m3fn_x4"),
    "ns": ("sbuf", [128, 128], "uint8"),
    "yb": ("sbuf", [128, 128], "float32"),
    "gw1q": ("sbuf", [128, 256], "float8_e4m3fn_x4"),
    "gw1s": ("sbuf", [128, 256], "uint8"),
    "gxq": ("sbuf", [128, 128], "float8_e4m3fn_x4"),
    "gxs": ("sbuf", [128, 128], "uint8"),
    "ps": ("psum", [128, 512 * 8], "float32"),
}
SEMAPHORES = (["ld_w1", "ld_w2", "qw1", "qw2", "zarr", "add", "z0", "z1", "a0", "a1", "a2", "a3", "qh", "nb",
               "ymm", "ycp", "st_h", "st_y", "sentA", "sentB", "sentC", "sentD", "ldxt", "qxt", "hpiece", "gift", "rsum",
               "ld_w1b", "qw1b", "arh"]
              + ["ldx%d" % r for r in range(5)] + ["qx%d" % r for r in range(5)]
              + ["mm%d_%d" % (r, i) for r in range(5) for i in range(2)]
              + ["cpa%d" % c for c in range(N)] + ["cpb%d" % c for c in range(N)]
              + ["arr%d" % c for c in range(N)])


def _count(mask):
    return bin(mask).count("1")


def _plan(cores, topo):
    n = len(cores)
    q = [r for r in range(n) if not any(topo.may_write(cores[r], cores[j]) for j in range(n) if j != r)][0]
    p = (q + 1) % n
    rest = [j for j in range(n) if j != q]
    free = [c for c in range(NCORES) if c not in cores]
    qc = cores[q]
    K = [c for c in free if topo.mates(topo.chip(c), topo.chip(qc)) and topo.may_write(c, qc)
         and topo.die(c) == topo.die(cores[rest[0]]) and all(topo.may_write(cores[j], c) for j in rest)][0]
    L = [c for c in free if topo.chip(c) == topo.chip(cores[p]) and topo.may_write(c, qc)
         and topo.die(c) == topo.die(cores[p])][0]
    own = [c for c in free if topo.chip(c) == topo.chip(qc) and topo.may_write(c, K)
           and all(topo.may_write(c, cores[j]) for j in rest)]
    near = [c for c in own if topo.die(c) == topo.die(qc)]
    far = [c for c in own if topo.die(c) != topo.die(qc)]
    relays = []
    for a, b in zip(near, far):
        relays += [a, b]
    place = {c: cores[c] for c in range(n)}
    place[q], place[p] = K, L
    ring = [j for j in rest if j != p]
    taker = {ring[k]: ring[(k + 1) % len(ring)] for k in range(len(ring))}
    giver = {t: a for a, t in taker.items()}
    helpers = {a: [c for c in free if c not in (K, L) and c not in relays and topo.chip(c) == topo.chip(cores[a])
                   and topo.die(c) != topo.die(cores[a]) and topo.may_write(c, cores[taker[a]])][:4] for a in ring}
    r0, r1, r2, r3 = ring
    order = {r0: [q, p, r3, r2], r1: [p, q, r0, r3], r2: [r1, q, p, r0], r3: [r2, p, q, r1],
             p: [q, r0, p, r3, r1, r2], q: [q] + [(q + s) % n for s in range(1, n)]}
    relay_of = {c: relays[k % len(relays)] for k, c in enumerate(order[q])}
    arrive = {}
    for c in range(n):
        ev = []
        for j in range(n):
            if c in order[j]:
                k = order[j].index(c)
                ev.append((0.5 * k + 2.5 if j == q else (2.5 if (j == p and c == q) else float(k)), j))
        arrive[c] = [j for _, j in sorted(ev)]
    arrive[q] = [j for j in arrive[q] if j not in (p, q)] + [p, q]
    return q, p, K, L, relays, place, order, relay_of, arrive, taker, giver, helpers


def _runs(tiles):
    groups = [tiles[0:1], tiles[1:3], tiles[3:]]
    out = []
    for gr in groups:
        s = sorted(gr)
        rs, cur = [], []
        for t in s:
            if cur and t != cur[-1] + 1:
                rs.append(cur)
                cur = []
            cur.append(t)
        if cur:
            rs.append(cur)
        rs.sort(key=lambda r: min(gr.index(t) for t in r))
        out += [(r, [t for t in gr if t in r]) for r in rs]
    return out


def rank_program(g, core, T, topo):
    cores = list(T.cores)
    q, p, K, L, relays, place, order, relay_of, arrive, taker, giver, helpers = _plan(cores, topo)
    rank = T.rank_of(core)
    piece_of = {h: (a, k) for a in helpers for k, h in enumerate(helpers[a])}
    if rank is None and core not in (K, L) and core not in relays and core not in piece_of:
        return
    V, S, TE, SY = g.vector, g.scalar, g.tensor, g.sync
    sem = T.sem
    sent = {"sentA": 0, "sentB": 0, "sentC": 0, "sentD": 0}

    def write(dst, out, in_, rsem, lsem, mask=None):
        rid, pid, _ = topo.addr(dst)
        m = topo.mask(core, dst) if mask is None else mask
        g.remote_dma(out_ap=out, in_ap=in_, remote_sem=rsem, local_sem=sem[lsem], pid=pid, routing_id=rid,
                     dma_engine_mask=m)
        sent[lsem] += _count(m)

    def slot(buf, c):
        return buf[:, W * c:W * c + W]

    def half(buf, c, i):
        return buf[:, W * c + 128 * i:W * c + 128 * i + 128]

    def in_count(src, dst, mask=None):
        return _count(topo.mask(src, dst) if mask is None else mask)

    def finish_g():
        for k in ("sentA", "sentB", "sentC", "sentD"):
            if sent[k]:
                g.wait_ge(sem[k], sent[k])

    off_mask = topo.mask(cores[p], K)
    chip_only = topo.mask(cores[p], L) & ~off_mask
    lanes = [chip_only, off_mask]

    def lane_of(k, i=0):
        return lanes[i] if k == 0 else lanes[(k + 1) % 2]

    def arrival_count(c, j):
        if j == q:
            return in_count(relay_of[c], place[c]) * (2 if c == order[q][0] else 1)
        if j == p and c == p:
            return _count(chip_only)
        if j == p and c == q:
            return in_count(L, K)
        return in_count(cores[j], place[c])

    def make_tile(z, w0, w1):
        for s_, v_ in w0:
            S.wait_ge(s_, v_)
        S.activation(T.ht[:, 0:512:4], z[:, 0:128], ActivationFunctionType.Relu, scale=CACT).then_inc(sem.a0, 1)
        S.activation(T.ht[:, 1:512:4], z[:, 0:128], ActivationFunctionType.Relu, scale=-CACT).then_inc(sem.a1, 1)
        for s_, v_ in w1:
            S.wait_ge(s_, v_)
            V.wait_ge(s_, v_)
        V.tensor_scalar(T.ht[:, 2:512:4], z[:, 128:256], 0.0, CACT, AluOpType.max, AluOpType.mult).then_inc(sem.a2, 1)
        S.activation(T.ht[:, 3:512:4], z[:, 128:256], ActivationFunctionType.Relu, scale=-CACT).then_inc(sem.a3, 1)
        for a in (sem.a0, sem.a1, sem.a2, sem.a3):
            V.wait_ge(a, 1)
        V.quantize_mx(T.hq[:, 0:128], T.hs[:, 0:128], T.ht[:, 0:512]).then_inc(sem.qh, 1)

    def sum_tile(c, last_psum=None):
        src = arrive[c]
        n_land = len(src) if last_psum else len(src) - 1
        done = 0
        for k in range(1, n_land):
            if k == 1:
                V.wait_ge(sem["arr%d" % src[0]], arrival_count(c, src[0]))
            V.wait_ge(sem["arr%d" % src[k]], arrival_count(c, src[k]))
            if done:
                V.wait_ge(sem.add, done)
            a = slot(T.land, src[0]) if k == 1 else T.acc[:, 0:W]
            V.tensor_tensor(T.acc[:, 0:W], a, slot(T.land, src[k]), AluOpType.add).then_inc(sem.add, 1)
            done += 1
        V.wait_ge(sem.add, done)
        if last_psum:
            halves, waits = last_psum
        else:
            j = src[-1]
            halves = (T.land[:, W * j:W * j + 128], T.land[:, W * j + 128:W * j + W])
            waits = ((sem["arr%d" % j], arrival_count(c, j)),) * 2
        for i, zs in enumerate((sem.z0, sem.z1)):
            V.wait_ge(waits[i][0], waits[i][1])
            V.tensor_tensor(T.acc[:, 128 * i:128 * i + 128], T.acc[:, 128 * i:128 * i + 128], halves[i],
                            AluOpType.add).then_inc(zs, 1)
        make_tile(T.acc, [(sem.z0, 1)], [(sem.z1, 1)])

    def close_q(base, own):
        V.tensor_tensor(T.acc2[:, 0:W], base, slot(T.land, p), AluOpType.add).then_inc(sem.rsum, 1)
        V.wait_ge(sem.rsum, 1)
        for s_, v_ in own[1]:
            V.wait_ge(s_, v_)
        for i, zs in enumerate((sem.z0, sem.z1)):
            V.tensor_tensor(T.acc2[:, 128 * i:128 * i + 128], T.acc2[:, 128 * i:128 * i + 128],
                            own[0][:, 128 * i:128 * i + 128], AluOpType.add).then_inc(zs, 1)
        make_tile(T.acc2, [(sem.z0, 1)], [(sem.z1, 1)])

    def send_codes(dst, lsem):
        g.wait_ge(sem.qh, 1)
        write(dst, T.nq[:, 0:128].bitcast(dt.uint8), T.hq[:, 0:128].bitcast(dt.uint8), sem.nb, lsem)
        write(dst, T.ns[:, 0:128], T.hs[:, 0:128], sem.nb, lsem)

    def pieces(xcol):
        return [(T.gw1q[:, 0:256].bitcast(dt.uint8), T.w1q[:, 0:256].bitcast(dt.uint8)),
                (T.gw1s[:, 0:256], T.w1s[:, 0:256]),
                (T.gxq[:, 0:128].bitcast(dt.uint8), T.xq[:, xcol:xcol + 128].bitcast(dt.uint8)),
                (T.gxs[:, 0:128], T.xs[:, xcol:xcol + 128])]

    if core in piece_of:
        a, k = piece_of[core]
        buf = pieces(0)[k][0]
        g.wait_ge(sem.hpiece, _count(chip_only))
        write(cores[taker[a]], buf, buf, sem.gift, "sentB")
        finish_g()
        return

    if core in relays:
        for k, c in enumerate(order[q]):
            if relay_of[c] == core:
                if k == 0:
                    g.wait_ge(sem.arh, _count(lane_of(0, 0)))
                    write(place[c], half(T.land, q, 0), half(T.land, c, 0), sem["arr%d" % q], "sentB")
                    g.wait_ge(sem["arr%d" % c], _count(lane_of(0, 1)))
                    write(place[c], half(T.land, q, 1), half(T.land, c, 1), sem["arr%d" % q], "sentB")
                else:
                    g.wait_ge(sem["arr%d" % c], _count(lane_of(k)))
                    write(place[c], slot(T.land, q), slot(T.land, c), sem["arr%d" % q], "sentB")
        finish_g()
        return

    if core == K:
        src = arrive[q][:-2]
        for k in range(1, len(src)):
            if k == 1:
                V.wait_ge(sem["arr%d" % src[0]], arrival_count(q, src[0]))
            V.wait_ge(sem["arr%d" % src[k]], arrival_count(q, src[k]))
            if k > 1:
                V.wait_ge(sem.add, k - 1)
            a = slot(T.land, src[0]) if k == 1 else T.acc[:, 0:W]
            V.tensor_tensor(T.acc[:, 0:W], a, slot(T.land, src[k]), AluOpType.add).then_inc(sem.add, 1)
        g.wait_ge(sem.add, len(src) - 1)
        write(cores[q], T.zin[:, 0:W], T.acc[:, 0:W], sem.zarr, "sentB", off_mask)
        V.wait_ge(sem.add, len(src) - 1)
        V.wait_ge(sem["arr%d" % p], arrival_count(q, p))
        close_q(T.acc[:, 0:W], (slot(T.land, q), [(sem["arr%d" % q], arrival_count(q, q))]))
        send_codes(cores[(q - 1) % N], "sentB")
        finish_g()
        return

    if core == L:
        c = p
        g.wait_ge(sem.zarr, _count(chip_only))
        write(K, slot(T.land, p), T.zin[:, 0:W], sem["arr%d" % p], "sentB")
        write(cores[q], slot(T.land, p), T.zin[:, 0:W], sem["arr%d" % p], "sentB")
        sum_tile(c)
        g.wait_ge(sem.z0, 1)
        g.wait_ge(sem.z1, 1)
        write(cores[c], T.zin[:, 0:W], T.acc[:, 0:W], sem.zarr, "sentB", off_mask)
        send_codes(cores[(c - 1) % N], "sentB")
        finish_g()
        return

    summed_here = place[rank] == core
    tiles = order[rank]
    runs = _runs(tiles)
    if summed_here:
        runs = runs + [([rank], [])]
    n_first = len(runs) - (1 if summed_here else 0)

    def load_x(queue, r):
        a, b = runs[r][0][0], runs[r][0][-1] + 1
        queue.dma_start(T.xb[:, 512 * a:512 * b], T.x[:, 512 * a:512 * b]).then_inc(sem["ldx%d" % r], 16)

    if rank == q:
        SY.dma_start(T.w1b[:, 0:512], T.w1[:, 0:512]).then_inc(sem.ld_w1, 16)
        load_x(S, 0)
        SY.dma_start(T.w1b[:, 512:1024], T.w1[:, 512:1024]).then_inc(sem.ld_w1b, 16)
        for r in range(1, len(runs)):
            load_x(S if r % 2 == 1 else SY, r)
    else:
        SY.dma_start(T.w1b[:, 0:1024], T.w1[:, 0:1024]).then_inc(sem.ld_w1, 16)
        if summed_here:
            t = taker[rank]
            S.dma_start(T.xb[:, 512 * t:512 * t + 512], T.x[:, 512 * t:512 * t + 512]).then_inc(sem.ldxt, 16)
        for r in range(len(runs)):
            load_x((S if r % 2 == 0 else SY) if not summed_here else (SY if r % 2 == 0 else S), r)

    readers = {}
    bank = {}

    def quant_run(r):
        a, b = runs[r][0][0], runs[r][0][-1] + 1
        V.wait_ge(sem["ldx%d" % r], 16)
        V.quantize_mx(T.xq[:, 128 * a:128 * b], T.xs[:, 128 * a:128 * b], T.xb[:, 512 * a:512 * b]).then_inc(sem["qx%d" % r], 1)

    def mult_run(r):
        a, b = runs[r][0][0], runs[r][0][-1] + 1
        TE.wait_ge(sem["qx%d" % r], 1)
        for i in range(2):
            bk = (2 * r + i) % 8
            for s_ in readers.get(bk, []):
                TE.wait_ge(s_, 1)
            readers[bk] = []
            bank[(r, i)] = bk
            if rank == q and i == 1:
                TE.wait_ge(sem.qw1b, 1)
            TE.matmul_mx(T.ps[:, 512 * bk:512 * bk + 128 * (b - a)], T.w1q[:, 128 * i:128 * i + 128],
                         T.w1s[:, 128 * i:128 * i + 128], T.xq[:, 128 * a:128 * b], T.xs[:, 128 * a:128 * b],
                         True, True).then_inc(sem["mm%d_%d" % (r, i)], 1)

    V.wait_ge(sem.ld_w1, 16)
    if rank == q:
        V.quantize_mx(T.w1q[:, 0:128], T.w1s[:, 0:128], T.w1b[:, 0:512]).then_inc(sem.qw1, 1)
        quant_run(0)
        V.wait_ge(sem.ld_w1b, 16)
        V.quantize_mx(T.w1q[:, 128:256], T.w1s[:, 128:256], T.w1b[:, 512:1024]).then_inc(sem.qw1b, 1)
    else:
        V.quantize_mx(T.w1q[:, 0:256], T.w1s[:, 0:256], T.w1b[:, 0:1024]).then_inc(sem.qw1, 1)
    TE.wait_ge(sem.qw1, 1)
    if summed_here:
        t = taker[rank]
        V.wait_ge(sem.ldxt, 16)
        V.quantize_mx(T.xq[:, 128 * t:128 * t + 128], T.xs[:, 128 * t:128 * t + 128],
                      T.xb[:, 512 * t:512 * t + 512]).then_inc(sem.qxt, 1)
        g.wait_ge(sem.qw1, 1)
        gift = pieces(128 * t)
        for k in (0, 2, 1, 3):
            if k == 2:
                g.wait_ge(sem.qxt, 1)
            write(helpers[rank][k], gift[k][0], gift[k][1], sem.hpiece, "sentD", chip_only)
    for r in range(n_first):
        early = rank == q and r == 0
        if not early:
            quant_run(r)
        mult_run(r)
        (S if early else V).wait_ge(sem["mm%d_0" % r], 1)
        if not early:
            S.wait_ge(sem["mm%d_1" % r], 1)
        for c in runs[r][1]:
            o = 128 * (c - runs[r][0][0])
            b0, b1 = bank[(r, 0)], bank[(r, 1)]
            if early:
                S.activation(T.sb[:, W * c:W * c + 128], T.ps[:, 512 * b0 + o:512 * b0 + o + 128],
                             ActivationFunctionType.Copy).then_inc(sem["cpa%d" % c], 1)
                S.wait_ge(sem["mm%d_1" % r], 1)
            else:
                V.tensor_copy(T.sb[:, W * c:W * c + 128], T.ps[:, 512 * b0 + o:512 * b0 + o + 128]).then_inc(sem["cpa%d" % c], 1)
            S.activation(T.sb[:, W * c + 128:W * c + W], T.ps[:, 512 * b1 + o:512 * b1 + o + 128],
                         ActivationFunctionType.Copy).then_inc(sem["cpb%d" % c], 1)
            readers[b0].append(sem["cpa%d" % c])
            readers[b1].append(sem["cpb%d" % c])

    for k, c in enumerate(tiles):
        ls = "sentA" if k < len(tiles) - 2 else "sentB"
        g.wait_ge(sem["cpa%d" % c], 1)
        if rank == q and k == 0:
            write(relay_of[c], half(T.land, c, 0), half(T.sb, c, 0), sem.arh, ls, lane_of(0, 0))
            g.wait_ge(sem["cpb%d" % c], 1)
            write(relay_of[c], half(T.land, c, 1), half(T.sb, c, 1), sem["arr%d" % c], ls, lane_of(0, 1))
            continue
        g.wait_ge(sem["cpb%d" % c], 1)
        if rank == q:
            write(relay_of[c], slot(T.land, c), slot(T.sb, c), sem["arr%d" % c], ls, lane_of(k))
        elif rank == p and c == q:
            write(L, T.zin[:, 0:W], slot(T.sb, c), sem.zarr, ls, chip_only)
        elif c == rank:
            write(place[c], slot(T.land, rank), slot(T.sb, c), sem["arr%d" % rank], ls, chip_only)
        else:
            write(place[c], slot(T.land, rank), slot(T.sb, c), sem["arr%d" % rank], ls)

    SY.wait_ge(sem.sentA, sent["sentA"])
    SY.dma_start(T.w2b[:, 0:1024], T.w2[:, 0:1024]).then_inc(sem.ld_w2, 16)

    def quant_w2():
        V.wait_ge(sem.ld_w2, 16)
        V.quantize_mx(T.w2q[:, 0:256], T.w2s[:, 0:256], T.w2b[:, 0:1024]).then_inc(sem.qw2, 1)

    if summed_here:
        r = n_first
        quant_run(r)
        TE.wait_ge(sem["qx%d" % r], 1)
        for i in range(2):
            bk = (2 * r + i) % 8
            for s_ in readers.get(bk, []):
                TE.wait_ge(s_, 1)
            readers[bk] = []
            bank[(r, i)] = bk
            TE.matmul_mx(T.ps[:, 512 * bk:512 * bk + 128], T.w1q[:, 128 * i:128 * i + 128], T.w1s[:, 128 * i:128 * i + 128],
                         T.xq[:, 128 * rank:128 * rank + 128], T.xs[:, 128 * rank:128 * rank + 128], True, False)
        TE.wait_ge(sem.gift, sum(in_count(h_, core) for h_ in helpers[giver[rank]]))
        for i in range(2):
            bk = bank[(r, i)]
            TE.matmul_mx(T.ps[:, 512 * bk:512 * bk + 128], T.gw1q[:, 128 * i:128 * i + 128], T.gw1s[:, 128 * i:128 * i + 128],
                         T.gxq[:, 0:128], T.gxs[:, 0:128], False, True).then_inc(sem["mm%d_%d" % (r, i)], 1)
        b0, b1 = bank[(r, 0)], bank[(r, 1)]
        sum_tile(rank,
                 last_psum=((T.ps[:, 512 * b0:512 * b0 + 128], T.ps[:, 512 * b1:512 * b1 + 128]),
                            ((sem["mm%d_0" % r], 1), (sem["mm%d_1" % r], 1))))
        quant_w2()
        send_codes(cores[(rank - 1) % N], "sentC")
    elif rank == q:
        quant_w2()
        V.wait_ge(sem.zarr, _count(off_mask))
        V.wait_ge(sem["arr%d" % p], in_count(L, core))
        close_q(T.zin[:, 0:W], (slot(T.sb, q), [(sem["cpa%d" % q], 1), (sem["cpb%d" % q], 1)]))
    else:
        quant_w2()
        n_z = _count(off_mask)
        make_tile(T.zin, [(sem.zarr, n_z)], [(sem.zarr, n_z)])

    for a in (sem.a0, sem.a1, sem.a2, sem.a3):
        SY.wait_ge(a, 1)
    if sent["sentC"]:
        SY.wait_ge(sem.sentC, sent["sentC"])
    SY.dma_start(T.h[:, 0:512], T.ht[:, 0:512]).then_inc(sem.st_h, 16)

    yb = (2 * len(runs)) % 8
    for s_ in readers.get(yb, []):
        TE.wait_ge(s_, 1)
    nxt = (rank + 1) % N
    src = K if nxt == q else (L if nxt == p else cores[nxt])
    TE.wait_ge(sem.qw2, 1)
    TE.wait_ge(sem.qh, 1)
    TE.matmul_mx(T.ps[:, 512 * yb:512 * yb + 128], T.w2q[:, 0:128], T.w2s[:, 0:128], T.hq[:, 0:128], T.hs[:, 0:128],
                 True, False)
    TE.wait_ge(sem.nb, 2 * in_count(src, core))
    TE.matmul_mx(T.ps[:, 512 * yb:512 * yb + 128], T.w2q[:, 128:256], T.w2s[:, 128:256], T.nq[:, 0:128], T.ns[:, 0:128],
                 False, True).then_inc(sem.ymm, 1)
    S.wait_ge(sem.ymm, 1)
    S.activation(T.yb[:, 0:128], T.ps[:, 512 * yb:512 * yb + 128], ActivationFunctionType.Copy).then_inc(sem.ycp, 1)
    S.wait_ge(sem.ycp, 1)
    S.dma_start(T.y[:, 0:128], T.yb[:, 0:128]).then_inc(sem.st_y, 16)

    finish_g()
    g.wait_ge(sem.st_h, 16)
    g.wait_ge(sem.st_y, 16)
